import numpy as np
import ml_dtypes


def mxq(x, axis, fmt="e4m3"):
    dtype, down = {"e4m3": (ml_dtypes.float8_e4m3fn, 7), "e5m2": (ml_dtypes.float8_e5m2, 14)}[fmt]
    v = np.moveaxis(np.asarray(x, np.float32).astype(ml_dtypes.bfloat16).astype(np.float64), axis, -1)
    blocks = v.reshape(v.shape[:-1] + (-1, 32))
    amax = np.abs(blocks).max(-1, keepdims=True)
    byte = np.maximum(np.where(amax > 0, np.frexp(amax)[1] - 1 + 127, 0) - down, 1)
    scale = np.exp2(byte - 127.0)
    codes = (blocks / scale).astype(np.float32).astype(dtype).astype(np.float64)
    return np.moveaxis((codes * scale).reshape(v.shape), -1, axis)


WIDE = False


def mx_kscale(k):
    if not WIDE:
        return np.ones(k)
    levels = np.array([10, -10, 5, -5, 0])
    if k % 512:
        return np.exp2(np.random.permutation(np.resize(levels, k // 32))).repeat(32)
    a = np.empty((k // 512, 16))
    for p in range(k // 512):
        a[p, :8] = np.random.permutation(np.resize(levels, 8))
        for g in range(8):
            far = levels[np.abs(levels - a[p, g]) >= 10]
            a[p, g + 8] = far[np.random.randint(len(far))]
    return np.exp2(a.ravel()).repeat(32)


def f64(x):
    return np.asarray(x).astype(np.float64)


def striped8(idx):
    return np.asarray(idx).reshape(8, -1, 16).transpose(0, 2, 1).reshape(128, -1).astype(np.uint16)


def unstriped8(offs):
    return offs.reshape(8, 16, -1).transpose(0, 2, 1).reshape(8, -1).astype(np.int64)


def pick8(x, idx, run):
    r = np.arange(len(x))
    return x[r[:, None], idx[r % (8 * run) // run]]


E2M1 = np.array([0.0, 0.5, 1.0, 1.5, 2.0, 3.0, 4.0, 6.0, -0.0, -0.5, -1.0, -1.5, -2.0, -3.0, -4.0, -6.0])


def pack_weight(w, fmt):
    k, n = w.shape
    w = f64(np.asarray(w, np.float32).astype(ml_dtypes.bfloat16)).reshape(k // 32, 32, n)
    amax = np.abs(w).max(1)
    if fmt == "e4m3":
        byte = np.frexp(amax)[1] - 1 + 127 - 7
    else:
        mant, ex = np.frexp(amax / 6.0)
        byte = np.where(mant > 0.5, ex, ex - 1) + 127
    byte = np.clip(np.where(amax > 0, byte, 1), 1, 254)
    scaled = (w * np.exp2(127.0 - byte)[:, None, :]).reshape(k, n).astype(np.float32)
    by_word = np.ascontiguousarray(scaled.reshape(k // 512, 128, 4, n).transpose(0, 1, 3, 2))
    if fmt == "e4m3":
        words = by_word.astype(ml_dtypes.float8_e4m3fn).view(np.uint8)
    else:
        c = by_word.astype(ml_dtypes.float4_e2m1fn).view(np.uint8) & 0xF
        words = (c[..., 0::2] | (c[..., 1::2] << 4)).reshape(k // 512, 128, 2 * n)
    return np.ascontiguousarray(words), np.ascontiguousarray(byte.astype(np.uint8).reshape(k // 512, 16, n))


def unpack_weight(words, scales, fmt):
    g, _, n = scales.shape
    words = np.ascontiguousarray(words).reshape(g, 128, n, -1)
    if fmt == "e4m3":
        vals = words.view(ml_dtypes.float8_e4m3fn).astype(np.float64)
    else:
        nib = np.empty((g, 128, n, 4), np.uint8)
        nib[..., 0::2] = words & 0xF
        nib[..., 1::2] = words >> 4
        vals = E2M1[nib]
    vals = vals * np.repeat(np.exp2(scales.astype(np.float64) - 127.0), 8, axis=1)[..., None]
    return vals.transpose(0, 1, 3, 2).reshape(g * 512, n)


def sigmoid(v):
    return 1.0 / (1.0 + np.exp(-v))


D, T, I, Q = 512, 1024, 512, 128


def setup_inputs():
    n = np.random.standard_normal
    idx = np.stack([np.random.permutation(T)[:I] for _ in range(8)])
    idx2 = np.stack([np.random.permutation(T)[:I] for _ in range(8)])
    idx3 = np.stack([np.random.permutation(T)[:I] for _ in range(8)])
    fd = mx_kscale(D)
    keysp = pack_weight(n((D, T)) / fd[:, None], "e2m1")
    return {
        "query": (n((D, Q)) * 1.5 / np.sqrt(D) * fd[:, None]).astype(np.float32),
        "keys_words": keysp[0],
        "keys_scales": keysp[1],
        "lam": (np.random.uniform(4.0, 9.0, (Q, 1))).astype(np.float32),
        "earlier": (np.random.uniform(0.1, 2.0, (Q, I))).astype(np.float32),
        "trust": (np.random.uniform(0.3, 0.8, (Q, 1))).astype(np.float32),
        "old": (np.random.uniform(0.0, 2.0, (Q, T))).astype(np.float32),
        "fade": (np.random.uniform(0.3, 0.9, (Q, 1))).astype(np.float32),
        "offs": striped8(idx),
        "offs2": striped8(idx2),
        "offs3": striped8(idx3),
    }


def reference(query, keys_words, keys_scales, lam, earlier, trust, old, fade, offs, offs2, offs3):
    idx = unstriped8(offs)
    idx2 = unstriped8(offs2)
    idx3 = unstriped8(offs3)
    keysu = unpack_weight(keys_words, keys_scales, "e2m1")
    queryq = mxq(f64(query), 0, "e4m3")
    a = queryq.T @ keysu
    s = sigmoid(pick8(a, idx, 16)) * sigmoid(pick8(a, idx2, 16)) * sigmoid(pick8(a, idx3, 16)) * f64(lam)
    p = np.exp(s - np.max(s, axis=1, keepdims=True))
    r = p / np.sum(p, axis=1, keepdims=True)
    re0 = f64(earlier) / np.sum(f64(earlier), axis=1, keepdims=True)
    w = r * f64(trust) + re0 * (1.0 - f64(trust))
    ws = w * 512.0
    wf = np.zeros((Q, T))
    wf[np.arange(Q)[:, None], idx[np.arange(Q) % 128 // 16]] = ws
    y = f64(old) * f64(fade) + wf
    return y

@@ -1,0 +1,149 @@
+from contextlib import ExitStack
+
+import concourse.mybir as mybir
+
+D, T, I, Q = 512, 1024, 512, 128
+FLOPS = 2 * D * Q * T
+
+F32 = mybir.dt.float32
+BF16 = mybir.dt.bfloat16
+I32 = mybir.dt.int32
+U32 = mybir.dt.uint32
+U16 = mybir.dt.uint16
+U8 = mybir.dt.uint8
+FP8X4 = mybir.dt.float8_e4m3fn_x4
+FP4X4 = mybir.dt.float4_e2m1fn_x4
+ALU = mybir.AluOpType
+ACT = mybir.ActivationFunctionType
+
+P = 128
+PACK = 4
+N_MM = 256
+HALF = I // 2
+OUT_COLS = 256
+
+
+def tile_attend_chainproduct_carried_counts_heads_kernel(
+    tc, query, keys_words, keys_scales, lam, earlier, trust, old, fade, offs, offs2, offs3, out
+):
+    nc = tc.nc
+    with ExitStack() as ctx:
+        lists = ctx.enter_context(tc.tile_pool(name="lists", bufs=1))
+        sb = ctx.enter_context(tc.tile_pool(name="sb", bufs=1))
+        psum = ctx.enter_context(tc.psum_pool(name="psum", bufs=1))
+
+        k_scales = sb.tile([P, T], U8, name="k_scales", align_bytes=64)
+        nc.vector.memset(k_scales[:].bitcast(I32), 0)
+
+        q_raw = sb.tile([P, PACK, Q], F32, name="q_raw")
+        nc.sync.dma_start(out=q_raw[:], in_=query.rearrange("(p j) w -> p j w", j=PACK))
+        k_words = sb.tile([P, 2 * T], U8, name="k_words", align_bytes=64)
+        nc.sync.dma_start(out=k_words[:].bitcast(I32), in_=keys_words[0].bitcast(I32))
+        list_a = lists.tile([P, I // 16], U16, name="list_a")
+        nc.sync.dma_start(list_a[:], offs)
+        scale_rows = keys_scales[0].bitcast(I32)
+        for quad in range(4):
+            nc.sync.dma_start(
+                out=k_scales[32 * quad : 32 * quad + 4, :].bitcast(I32),
+                in_=scale_rows[4 * quad : 4 * quad + 4, :],
+            )
+
+        list_b = lists.tile([P, I // 16], U16, name="list_b")
+        list_c = lists.tile([P, I // 16], U16, name="list_c")
+        earlier_sb = sb.tile([P, I], F32, name="earlier_sb")
+        nc.sync.dma_start(out=earlier_sb[:], in_=earlier)
+        nc.sync.dma_start(list_c[:], offs3)
+        nc.sync.dma_start(list_b[:], offs2)
+        lam_sb = sb.tile([P, 1], F32, name="lam_sb")
+        trust_sb = sb.tile([P, 1], F32, name="trust_sb")
+        fade_sb = sb.tile([P, 1], F32, name="fade_sb")
+        nc.sync.dma_start(out=lam_sb[:], in_=lam)
+        nc.sync.dma_start(out=trust_sb[:], in_=trust)
+        nc.sync.dma_start(out=fade_sb[:], in_=fade)
+
+        old_sb = sb.tile([P, T], F32, name="old_sb")
+        nc.sync.dma_start(out=old_sb[:], in_=old)
+
+        earlier_pairs = sb.tile([P, HALF], F32, name="earlier_pairs")
+        nc.gpsimd.tensor_tensor(earlier_pairs[:], earlier_sb[:, :HALF], earlier_sb[:, HALF:], ALU.add)
+
+        wf = sb.tile([P, T], F32, name="wf")
+        nc.vector.memset(wf[:], 0.0)
+
+        new_gain = sb.tile([P, 1], F32, name="new_gain")
+        old_gain = sb.tile([P, 1], F32, name="old_gain")
+        nc.gpsimd.tensor_scalar(new_gain[:], trust_sb[:], 512.0, 0.0, ALU.mult, ALU.add)
+        nc.gpsimd.tensor_scalar(old_gain[:], trust_sb[:], -512.0, 512.0, ALU.mult, ALU.add)
+
+        q_bf = sb.tile([P, Q, PACK], BF16, name="q_bf", align_bytes=64)
+        nc.vector.tensor_copy(out=q_bf[:], in_=q_raw[:].rearrange("p j w -> p w j"))
+        q_codes = sb.tile([P, Q], U32, name="q_codes", align_bytes=64)
+        q_scales = sb.tile([P, Q], U8, name="q_scales", align_bytes=64)
+        nc.vector.quantize_mx(
+            out=q_codes[:].bitcast(FP8X4), scales=q_scales[:], in_=q_bf[:].rearrange("p w j -> p (w j)")
+        )
+
+        a_sb = sb.tile([P, T], F32, name="a_sb")
+        for m, (c0, c1) in enumerate(((0, 256), (256, 512), (512, 768), (768, 896), (896, 1024))):
+            cols = slice(c0, c1)
+            acc = psum.tile([P, c1 - c0], F32, name="acc%d" % m)
+            nc.tensor.matmul_mx(
+                out=acc[:],
+                lhsT=q_codes[:].bitcast(FP8X4),
+                lhsT_scale=q_scales[:],
+                rhs=k_words[:, 2 * c0 : 2 * c1].bitcast(FP4X4),
+                rhs_scale=k_scales[:, cols],
+                start=True,
+                stop=True,
+            )
+            nc.vector.tensor_copy(out=a_sb[:, cols], in_=acc[:])
+
+        halves = [slice(h * HALF, (h + 1) * HALF) for h in range(2)]
+        list_halves = [slice(h * HALF // 16, (h + 1) * HALF // 16) for h in range(2)]
+
+        lo, hi = halves
+        gb = sb.tile([P, I], F32, name="gb")
+        gc_lo = sb.tile([P, HALF], F32, name="gc_lo")
+        sa = sb.tile([P, I], F32, name="sa")
+        sb2 = sb.tile([P, I], F32, name="sb2")
+        sc = sb.tile([P, I], F32, name="sc")
+        nc.vector.tensor_copy(gc_lo[:], a_sb[:].indirect(list_c[:, list_halves[0]]))
+        nc.vector.tensor_copy(gb[:], a_sb[:].indirect(list_b[:]))
+        nc.scalar.activation(sa[:], a_sb[:].indirect(list_a[:]), ACT.Sigmoid)
+        nc.scalar.activation(sc[:, hi], a_sb[:].indirect(list_c[:, list_halves[1]]), ACT.Sigmoid)
+        nc.scalar.activation(sc[:, lo], gc_lo[:], ACT.Sigmoid)
+        for h in (hi, lo):
+            nc.scalar.activation(sb2[:, h], gb[:, h], ACT.Sigmoid)
+
+        m2 = sb.tile([P, I], F32, name="m2")
+        u = sb.tile([P, I], F32, name="u")
+        neg_s = sb.tile([P, I], F32, name="neg_s")
+        low = sb.tile([P, 1], F32, name="low")
+        for h in (hi, lo):
+            nc.vector.scalar_tensor_tensor(m2[:, h], sa[:, h], -1.0, sc[:, h], ALU.mult, ALU.mult)
+        for h in (hi, lo):
+            nc.vector.tensor_tensor(u[:, h], m2[:, h], sb2[:, h], ALU.mult)
+        earlier_sum = m2[:, HALF : HALF + 1]
+        nc.vector.tensor_reduce(earlier_sum, earlier_pairs[:], mybir.AxisListType.X, ALU.add)
+        nc.vector.tensor_scalar(neg_s[:], u[:], lam_sb[:], None, ALU.mult, ALU.min, accum_out=low[:])
+
+        p = sb.tile([P, I], F32, name="p")
+        p_sum = sb.tile([P, 1], F32, name="p_sum")
+        nc.scalar.activation(p[:], neg_s[:], ACT.Exp, bias=low[:], scale=-1.0, accum_out=p_sum[:])
+
+        earlier_inv = sb.tile([P, 1], F32, name="earlier_inv")
+        nc.vector.reciprocal(earlier_inv[:], earlier_sum)
+        carried = u
+        nc.vector.tensor_scalar(carried[:], earlier_sb[:], earlier_inv[:], old_gain[:], ALU.mult, ALU.mult)
+        p_inv = sb.tile([P, 1], F32, name="p_inv")
+        nc.vector.reciprocal(p_inv[:], p_sum[:])
+        fresh = sb.tile([P, I], F32, name="fresh")
+        nc.vector.tensor_scalar(fresh[:], p[:], p_inv[:], new_gain[:], ALU.mult, ALU.mult)
+        nc.vector.tensor_tensor(wf[:].indirect(list_a[:]), fresh[:], carried[:], ALU.add)
+
+        for c in range(T // OUT_COLS):
+            cols = slice(c * OUT_COLS, (c + 1) * OUT_COLS)
+            y = sb.tile([P, OUT_COLS], F32, name="y%d" % c)
+            nc.vector.scalar_tensor_tensor(y[:], old_sb[:, cols], fade_sb[:], wf[:, cols], ALU.mult, ALU.add)
+            queue = nc.sync if c % 2 == 0 else nc.scalar
+            queue.dma_start(out=out[:, cols], in_=y[:])

@@ -50,10 +50,10 @@ def tile_attend_chainproduct_carried_counts_heads_kernel(
 
         list_b = lists.tile([P, I // 16], U16, name="list_b")
         list_c = lists.tile([P, I // 16], U16, name="list_c")
+        nc.sync.dma_start(list_b[:], offs2)
         earlier_sb = sb.tile([P, I], F32, name="earlier_sb")
         nc.sync.dma_start(out=earlier_sb[:], in_=earlier)
         nc.sync.dma_start(list_c[:], offs3)
-        nc.sync.dma_start(list_b[:], offs2)
         lam_sb = sb.tile([P, 1], F32, name="lam_sb")
         trust_sb = sb.tile([P, 1], F32, name="trust_sb")
         fade_sb = sb.tile([P, 1], F32, name="fade_sb")
@@ -76,7 +76,10 @@ def tile_attend_chainproduct_carried_counts_heads_kernel(
         nc.gpsimd.tensor_scalar(old_gain[:], trust_sb[:], -512.0, 512.0, ALU.mult, ALU.add)
 
         q_bf = sb.tile([P, Q, PACK], BF16, name="q_bf", align_bytes=64)
-        nc.vector.tensor_copy(out=q_bf[:], in_=q_raw[:].rearrange("p j w -> p w j"))
+        nc.vector.tensor_copy(
+            out=q_bf[:].rearrange("p (c i) j -> p c j i", i=4),
+            in_=q_raw[:].rearrange("p j (c i) -> p c j i", i=4),
+        )
         q_codes = sb.tile([P, Q], U32, name="q_codes", align_bytes=64)
         q_scales = sb.tile([P, Q], U8, name="q_scales", align_bytes=64)
         nc.vector.quantize_mx(
@@ -107,33 +110,32 @@ def tile_attend_chainproduct_carried_counts_heads_kernel(
         sa = sb.tile([P, I], F32, name="sa")
         sb2 = sb.tile([P, I], F32, name="sb2")
         sc = sb.tile([P, I], F32, name="sc")
-        nc.vector.tensor_copy(gc_lo[:], a_sb[:].indirect(list_c[:, list_halves[0]]))
         nc.vector.tensor_copy(gb[:], a_sb[:].indirect(list_b[:]))
+        nc.vector.tensor_copy(gc_lo[:], a_sb[:].indirect(list_c[:, list_halves[0]]))
         nc.scalar.activation(sa[:], a_sb[:].indirect(list_a[:]), ACT.Sigmoid)
         nc.scalar.activation(sc[:, hi], a_sb[:].indirect(list_c[:, list_halves[1]]), ACT.Sigmoid)
-        nc.scalar.activation(sc[:, lo], gc_lo[:], ACT.Sigmoid)
-        for h in (hi, lo):
+        for h in (lo, hi):
             nc.scalar.activation(sb2[:, h], gb[:, h], ACT.Sigmoid)
+        nc.scalar.activation(sc[:, lo], gc_lo[:], ACT.Sigmoid)
 
         m2 = sb.tile([P, I], F32, name="m2")
-        u = sb.tile([P, I], F32, name="u")
-        neg_s = sb.tile([P, I], F32, name="neg_s")
-        low = sb.tile([P, 1], F32, name="low")
-        for h in (hi, lo):
-            nc.vector.scalar_tensor_tensor(m2[:, h], sa[:, h], -1.0, sc[:, h], ALU.mult, ALU.mult)
-        for h in (hi, lo):
-            nc.vector.tensor_tensor(u[:, h], m2[:, h], sb2[:, h], ALU.mult)
+        score = sb.tile([P, I], F32, name="score")
+        neg_max = sb.tile([P, 1], F32, name="neg_max")
+        for h, second in ((hi, sc), (lo, sb2)):
+            nc.vector.scalar_tensor_tensor(m2[:, h], sa[:, h], lam_sb[:], second[:, h], ALU.mult, ALU.mult)
+        for h, third in ((hi, sb2), (lo, sc)):
+            nc.vector.tensor_tensor(score[:, h], m2[:, h], third[:, h], ALU.mult)
         earlier_sum = m2[:, HALF : HALF + 1]
         nc.vector.tensor_reduce(earlier_sum, earlier_pairs[:], mybir.AxisListType.X, ALU.add)
-        nc.vector.tensor_scalar(neg_s[:], u[:], lam_sb[:], None, ALU.mult, ALU.min, accum_out=low[:])
+        nc.vector.tensor_reduce(neg_max[:], score[:], mybir.AxisListType.X, ALU.max, negate=True)
 
         p = sb.tile([P, I], F32, name="p")
         p_sum = sb.tile([P, 1], F32, name="p_sum")
-        nc.scalar.activation(p[:], neg_s[:], ACT.Exp, bias=low[:], scale=-1.0, accum_out=p_sum[:])
+        nc.scalar.activation(p[:], score[:], ACT.Exp, bias=neg_max[:], accum_out=p_sum[:])
 
         earlier_inv = sb.tile([P, 1], F32, name="earlier_inv")
         nc.vector.reciprocal(earlier_inv[:], earlier_sum)
-        carried = u
+        carried = sb.tile([P, I], F32, name="carried")
         nc.vector.tensor_scalar(carried[:], earlier_sb[:], earlier_inv[:], old_gain[:], ALU.mult, ALU.mult)
         p_inv = sb.tile([P, 1], F32, name="p_inv")
         nc.vector.reciprocal(p_inv[:], p_sum[:])
@@ -141,9 +143,9 @@ def tile_attend_chainproduct_carried_counts_heads_kernel(
         nc.vector.tensor_scalar(fresh[:], p[:], p_inv[:], new_gain[:], ALU.mult, ALU.mult)
         nc.vector.tensor_tensor(wf[:].indirect(list_a[:]), fresh[:], carried[:], ALU.add)
 
-        for c in range(T // OUT_COLS):
-            cols = slice(c * OUT_COLS, (c + 1) * OUT_COLS)
-            y = sb.tile([P, OUT_COLS], F32, name="y%d" % c)
+        for c, (c0, c1) in enumerate(((0, 128), (128, 384), (384, 640), (640, 896), (896, 1024))):
+            cols = slice(c0, c1)
+            y = sb.tile([P, c1 - c0], F32, name="y%d" % c)
             nc.vector.scalar_tensor_tensor(y[:], old_sb[:, cols], fade_sb[:], wf[:, cols], ALU.mult, ALU.add)
             queue = nc.sync if c % 2 == 0 else nc.scalar
             queue.dma_start(out=out[:, cols], in_=y[:])

from contextlib import ExitStack

import concourse.mybir as mybir

D, T, I, Q = 512, 1024, 512, 128
FLOPS = 2 * D * Q * T

F32 = mybir.dt.float32
BF16 = mybir.dt.bfloat16
I32 = mybir.dt.int32
U32 = mybir.dt.uint32
U16 = mybir.dt.uint16
U8 = mybir.dt.uint8
FP8X4 = mybir.dt.float8_e4m3fn_x4
FP4X4 = mybir.dt.float4_e2m1fn_x4
ALU = mybir.AluOpType
ACT = mybir.ActivationFunctionType

P = 128
PACK = 4
N_MM = 256
HALF = I // 2
OUT_COLS = 256


def tile_attend_chainproduct_carried_counts_heads_kernel(
    tc, query, keys_words, keys_scales, lam, earlier, trust, old, fade, offs, offs2, offs3, out
):
    nc = tc.nc
    with ExitStack() as ctx:
        lists = ctx.enter_context(tc.tile_pool(name="lists", bufs=1))
        sb = ctx.enter_context(tc.tile_pool(name="sb", bufs=1))
        psum = ctx.enter_context(tc.psum_pool(name="psum", bufs=1))

        k_scales = sb.tile([P, T], U8, name="k_scales", align_bytes=64)
        nc.vector.memset(k_scales[:].bitcast(I32), 0)

        q_raw = sb.tile([P, PACK, Q], F32, name="q_raw")
        nc.sync.dma_start(out=q_raw[:], in_=query.rearrange("(p j) w -> p j w", j=PACK))
        k_words = sb.tile([P, 2 * T], U8, name="k_words", align_bytes=64)
        nc.sync.dma_start(out=k_words[:].bitcast(I32), in_=keys_words[0].bitcast(I32))
        list_a = lists.tile([P, I // 16], U16, name="list_a")
        nc.sync.dma_start(list_a[:], offs)
        scale_rows = keys_scales[0].bitcast(I32)
        for quad in range(4):
            nc.sync.dma_start(
                out=k_scales[32 * quad : 32 * quad + 4, :].bitcast(I32),
                in_=scale_rows[4 * quad : 4 * quad + 4, :],
            )

        list_b = lists.tile([P, I // 16], U16, name="list_b")
        list_c = lists.tile([P, I // 16], U16, name="list_c")
        nc.sync.dma_start(list_b[:], offs2)
        earlier_sb = sb.tile([P, I], F32, name="earlier_sb")
        nc.sync.dma_start(out=earlier_sb[:], in_=earlier)
        nc.sync.dma_start(list_c[:], offs3)
        lam_sb = sb.tile([P, 1], F32, name="lam_sb")
        trust_sb = sb.tile([P, 1], F32, name="trust_sb")
        fade_sb = sb.tile([P, 1], F32, name="fade_sb")
        nc.sync.dma_start(out=lam_sb[:], in_=lam)
        nc.sync.dma_start(out=trust_sb[:], in_=trust)
        nc.sync.dma_start(out=fade_sb[:], in_=fade)

        old_sb = sb.tile([P, T], F32, name="old_sb")
        nc.sync.dma_start(out=old_sb[:], in_=old)

        earlier_pairs = sb.tile([P, HALF], F32, name="earlier_pairs")
        nc.gpsimd.tensor_tensor(earlier_pairs[:], earlier_sb[:, :HALF], earlier_sb[:, HALF:], ALU.add)

        wf = sb.tile([P, T], F32, name="wf")
        nc.vector.memset(wf[:], 0.0)

        new_gain = sb.tile([P, 1], F32, name="new_gain")
        old_gain = sb.tile([P, 1], F32, name="old_gain")
        nc.gpsimd.tensor_scalar(new_gain[:], trust_sb[:], 512.0, 0.0, ALU.mult, ALU.add)
        nc.gpsimd.tensor_scalar(old_gain[:], trust_sb[:], -512.0, 512.0, ALU.mult, ALU.add)

        q_bf = sb.tile([P, Q, PACK], BF16, name="q_bf", align_bytes=64)
        nc.vector.tensor_copy(
            out=q_bf[:].rearrange("p (c i) j -> p c j i", i=4),
            in_=q_raw[:].rearrange("p j (c i) -> p c j i", i=4),
        )
        q_codes = sb.tile([P, Q], U32, name="q_codes", align_bytes=64)
        q_scales = sb.tile([P, Q], U8, name="q_scales", align_bytes=64)
        nc.vector.quantize_mx(
            out=q_codes[:].bitcast(FP8X4), scales=q_scales[:], in_=q_bf[:].rearrange("p w j -> p (w j)")
        )

        a_sb = sb.tile([P, T], F32, name="a_sb")
        for m, (c0, c1) in enumerate(((0, 256), (256, 512), (512, 768), (768, 896), (896, 1024))):
            cols = slice(c0, c1)
            acc = psum.tile([P, c1 - c0], F32, name="acc%d" % m)
            nc.tensor.matmul_mx(
                out=acc[:],
                lhsT=q_codes[:].bitcast(FP8X4),
                lhsT_scale=q_scales[:],
                rhs=k_words[:, 2 * c0 : 2 * c1].bitcast(FP4X4),
                rhs_scale=k_scales[:, cols],
                start=True,
                stop=True,
            )
            nc.vector.tensor_copy(out=a_sb[:, cols], in_=acc[:])

        halves = [slice(h * HALF, (h + 1) * HALF) for h in range(2)]
        list_halves = [slice(h * HALF // 16, (h + 1) * HALF // 16) for h in range(2)]

        lo, hi = halves
        gb = sb.tile([P, I], F32, name="gb")
        gc_lo = sb.tile([P, HALF], F32, name="gc_lo")
        sa = sb.tile([P, I], F32, name="sa")
        sb2 = sb.tile([P, I], F32, name="sb2")
        sc = sb.tile([P, I], F32, name="sc")
        nc.vector.tensor_copy(gb[:], a_sb[:].indirect(list_b[:]))
        nc.vector.tensor_copy(gc_lo[:], a_sb[:].indirect(list_c[:, list_halves[0]]))
        nc.scalar.activation(sa[:], a_sb[:].indirect(list_a[:]), ACT.Sigmoid)
        nc.scalar.activation(sc[:, hi], a_sb[:].indirect(list_c[:, list_halves[1]]), ACT.Sigmoid)
        for h in (lo, hi):
            nc.scalar.activation(sb2[:, h], gb[:, h], ACT.Sigmoid)
        nc.scalar.activation(sc[:, lo], gc_lo[:], ACT.Sigmoid)

        m2 = sb.tile([P, I], F32, name="m2")
        score = sb.tile([P, I], F32, name="score")
        neg_max = sb.tile([P, 1], F32, name="neg_max")
        for h, second in ((hi, sc), (lo, sb2)):
            nc.vector.scalar_tensor_tensor(m2[:, h], sa[:, h], lam_sb[:], second[:, h], ALU.mult, ALU.mult)
        for h, third in ((hi, sb2), (lo, sc)):
            nc.vector.tensor_tensor(score[:, h], m2[:, h], third[:, h], ALU.mult)
        earlier_sum = m2[:, HALF : HALF + 1]
        nc.vector.tensor_reduce(earlier_sum, earlier_pairs[:], mybir.AxisListType.X, ALU.add)
        nc.vector.tensor_reduce(neg_max[:], score[:], mybir.AxisListType.X, ALU.max, negate=True)

        p = sb.tile([P, I], F32, name="p")
        p_sum = sb.tile([P, 1], F32, name="p_sum")
        nc.scalar.activation(p[:], score[:], ACT.Exp, bias=neg_max[:], accum_out=p_sum[:])

        earlier_inv = sb.tile([P, 1], F32, name="earlier_inv")
        nc.vector.reciprocal(earlier_inv[:], earlier_sum)
        carried = sb.tile([P, I], F32, name="carried")
        nc.vector.tensor_scalar(carried[:], earlier_sb[:], earlier_inv[:], old_gain[:], ALU.mult, ALU.mult)
        p_inv = sb.tile([P, 1], F32, name="p_inv")
        nc.vector.reciprocal(p_inv[:], p_sum[:])
        fresh = sb.tile([P, I], F32, name="fresh")
        nc.vector.tensor_scalar(fresh[:], p[:], p_inv[:], new_gain[:], ALU.mult, ALU.mult)
        nc.vector.tensor_tensor(wf[:].indirect(list_a[:]), fresh[:], carried[:], ALU.add)

        for c, (c0, c1) in enumerate(((0, 128), (128, 384), (384, 640), (640, 896), (896, 1024))):
            cols = slice(c0, c1)
            y = sb.tile([P, c1 - c0], F32, name="y%d" % c)
            nc.vector.scalar_tensor_tensor(y[:], old_sb[:, cols], fade_sb[:], wf[:, cols], ALU.mult, ALU.add)
            queue = nc.sync if c % 2 == 0 else nc.scalar
            queue.dma_start(out=out[:, cols], in_=y[:])
